import numpy as np
import ml_dtypes


def mxq(x, axis, fmt="e4m3"):
    dtype, down = {"e4m3": (ml_dtypes.float8_e4m3fn, 7), "e5m2": (ml_dtypes.float8_e5m2, 14)}[fmt]
    v = np.moveaxis(np.asarray(x, np.float32).astype(ml_dtypes.bfloat16).astype(np.float64), axis, -1)
    blocks = v.reshape(v.shape[:-1] + (-1, 32))
    amax = np.abs(blocks).max(-1, keepdims=True)
    byte = np.maximum(np.where(amax > 0, np.frexp(amax)[1] - 1 + 127, 0) - down, 1)
    scale = np.exp2(byte - 127.0)
    codes = (blocks / scale).astype(np.float32).astype(dtype).astype(np.float64)
    return np.moveaxis((codes * scale).reshape(v.shape), -1, axis)


WIDE = False


def mx_kscale(k):
    if not WIDE:
        return np.ones(k)
    levels = np.array([10, -10, 5, -5, 0])
    if k % 512:
        return np.exp2(np.random.permutation(np.resize(levels, k // 32))).repeat(32)
    a = np.empty((k // 512, 16))
    for p in range(k // 512):
        a[p, :8] = np.random.permutation(np.resize(levels, 8))
        for g in range(8):
            far = levels[np.abs(levels - a[p, g]) >= 10]
            a[p, g + 8] = far[np.random.randint(len(far))]
    return np.exp2(a.ravel()).repeat(32)


def f64(x):
    return np.asarray(x).astype(np.float64)


def striped(idx):
    return np.tile(idx.reshape(-1, 16).T, (8, 1)).astype(np.uint16)


def unstriped(offs):
    return offs[:16].T.reshape(-1).astype(np.int64)


def gelu(v):
    return 0.5 * v * (1.0 + np.tanh(np.sqrt(2.0 / np.pi) * (v + 0.044715 * v**3)))


K, T, S, J, H, N = 512, 2048, 768, 512, 512, 256


def setup_inputs():
    n = np.random.standard_normal
    s = mx_kscale(K)[:, None]
    u = mx_kscale(H)
    r = mx_kscale(J)[:, None]
    return {
        "xT": (n((K, T)) * s).astype(np.float32),
        "eT": (n((J, S)) * r).astype(np.float32),
        "w1": (n((K, H)) / np.sqrt(K) / s * u).astype(np.float32),
        "w3": (n((J, H)) / np.sqrt(J) / r).astype(np.float32),
        "w2": (n((H, N)) / np.sqrt(H) / u[:, None]).astype(np.float32),
        "offs": striped(np.random.permutation(T)[:S]),
    }


def reference(xT, eT, w1, w3, w2, offs):
    c = mxq(f64(w1), 0, "e4m3").T @ mxq(f64(xT)[:, unstriped(offs)], 0, "e4m3")
    z = c * gelu(mxq(f64(w3), 0, "e4m3").T @ mxq(f64(eT), 0, "e4m3"))
    return mxq(f64(w2), 0, "e4m3").T @ mxq(z, 0, "e4m3")

@@ -1,0 +1,216 @@
+from contextlib import ExitStack
+
+import concourse.mybir as mybir
+
+K, T, S, J, H, N = 512, 2048, 768, 512, 512, 256
+FLOPS = 2 * S * (K * H + J * H + H * N)
+
+F32 = mybir.dt.float32
+BF16 = mybir.dt.bfloat16
+U32 = mybir.dt.uint32
+U16 = mybir.dt.uint16
+U8 = mybir.dt.uint8
+FP8X4 = mybir.dt.float8_e4m3fn_x4
+GELU = mybir.ActivationFunctionType.Gelu_apprx_tanh
+MULT = mybir.AluOpType.mult
+
+P = 128
+BLOCK = 128
+
+
+def tile_picked_schnet_gelu_e_kernel(tc, xT, eT, w1, w3, w2, offs, out):
+    nc = tc.nc
+    with ExitStack() as ctx:
+        keep = ctx.enter_context(tc.tile_pool(name="keep", bufs=1))
+        psum_f = ctx.enter_context(tc.psum_pool(name="psum_f", bufs=3))
+        psum_c = ctx.enter_context(tc.psum_pool(name="psum_c", bufs=3))
+        psum_o = ctx.enter_context(tc.psum_pool(name="psum_o", bufs=2))
+
+        offsets = keep.tile([P, S // 16], U16, name="offsets")
+        nc.sync.dma_start(offsets[:], offs)
+        x_rows = xT.rearrange("(p j) t -> p j t", j=4)
+        e_rows = eT.rearrange("(p j) s -> p j s", j=4)
+        weights = {"w1": w1, "w3": w3, "w2": w2}
+        raw, codes, scales, grouped, planes, e_raw = {}, {}, {}, {}, {}, {}
+        f_banks, c_banks, o_banks, gates = {}, {}, {}, {}
+
+        for name, width in (("x", S), ("e", S), ("z", S), ("w1", H), ("w3", H), ("w2", N)):
+            codes[name] = keep.tile([P, width], U32, name="codes_" + name, align_bytes=64)
+            scales[name] = keep.tile([P, width], U8, name="scales_" + name, align_bytes=64)
+            grouped[name] = keep.tile([P, width, 4], BF16, name="grouped_" + name, align_bytes=64)
+        picked = keep.tile([P, 4, S], F32, name="picked", align_bytes=64)
+
+        def load_plane(j):
+            planes[j] = keep.tile([P, T], F32, name="plane%d" % j, align_bytes=64)
+            nc.sync.dma_start(planes[j][:], x_rows[:, j, :])
+
+        def load_edges(a, b):
+            e_raw[a] = keep.tile([P, 4, b - a], F32, name="e_raw%d" % a, align_bytes=64)
+            nc.sync.dma_start(e_raw[a][:], e_rows[:, :, a:b])
+
+        def load_weights(name):
+            raw[name] = keep.tile([P, 4, weights[name].shape[1]], F32, name="raw_" + name, align_bytes=64)
+            nc.sync.dma_start(raw[name][:], weights[name].rearrange("(p j) h -> p j h", j=4))
+
+        def warm_table():
+            dummy = keep.tile([P, 1], F32, name="dummy")
+            nc.gpsimd.memset(dummy[:], 0.0)
+            dummy_out = keep.tile([P, 1], F32, name="dummy_out")
+            nc.scalar.activation(dummy_out[:], dummy[:], GELU)
+
+        def copy(engine, dst, src):
+            if engine == "S":
+                nc.scalar.copy(dst, src)
+            elif engine == "V":
+                nc.vector.tensor_copy(dst, src)
+            else:
+                nc.gpsimd.tensor_copy(dst, src)
+
+        def picks(a, b):
+            return offsets[:] if (a, b) == (0, S) else offsets[:, a // 16 : b // 16]
+
+        def gather(j, a, b):
+            nc.vector.tensor_copy(picked[:, j, a:b], planes[j][:].indirect(picks(a, b)))
+
+        def gather_wide(j):
+            nc.vector.tensor_copy(grouped["x"][:, :, j], planes[j][:].indirect(offsets[:]))
+
+        def group_x(engine, j0, j1, a, b):
+            copy(engine, grouped["x"][:, a:b, j0:j1], picked[:, j0:j1, a:b].rearrange("p j n -> p n j"))
+
+        def group_weights(name, engine, a, b):
+            if name == "w2":
+                copy(engine, grouped[name][:, a:b, :], raw[name][:, :, a:b].rearrange("p j n -> p n j"))
+            else:
+                dst = grouped[name][:].rearrange("p (t m) j -> p m t j", t=4)
+                src = raw[name][:].rearrange("p j (m t) -> p m t j", t=4)
+                copy(engine, dst[:, a:b], src[:, a:b])
+
+        def group_edges(engine, a, b):
+            start = max(s for s in e_raw if s <= a)
+            copy(engine, grouped["e"][:, a:b, :], e_raw[start][:, :, a - start : b - start].rearrange("p j n -> p n j"))
+
+        def quantise(name, a, b):
+            nc.vector.quantize_mx(
+                out=codes[name][:, a:b].bitcast(FP8X4),
+                scales=scales[name][:, a:b],
+                in_=grouped[name][:, a:b, :].rearrange("p w j -> p (w j)"),
+            )
+
+        def multiply(bank, w, t, x, a, b):
+            chans = slice(t * P, (t + 1) * P)
+            nc.tensor.matmul_mx(
+                out=bank,
+                lhsT=codes[w][:, chans].bitcast(FP8X4),
+                lhsT_scale=scales[w][:, chans],
+                rhs=codes[x][:, a:b].bitcast(FP8X4),
+                rhs_scale=scales[x][:, a:b],
+                start=True,
+                stop=True,
+            )
+
+        def filter_product(b):
+            f_banks[b] = psum_f.tile([P, 4, BLOCK], F32, name="f")
+            for t in range(4):
+                multiply(f_banks[b][:, t, :], "w3", t, "e", b * BLOCK, (b + 1) * BLOCK)
+
+        def atom_product(b):
+            c_banks[b] = psum_c.tile([P, 4, BLOCK], F32, name="c")
+            for t in range(4):
+                multiply(c_banks[b][:, t, :], "w1", t, "x", b * BLOCK, (b + 1) * BLOCK)
+
+        def gate(b):
+            gates[b] = keep.tile([P, BLOCK, 4], F32, name="gate%d" % b, align_bytes=64)
+            nc.scalar.activation(gates[b][:], f_banks[b][:].rearrange("p t n -> p n t"), GELU)
+
+        def message(b):
+            nc.vector.tensor_tensor(
+                grouped["z"][:, b * BLOCK : (b + 1) * BLOCK, :],
+                c_banks[b][:].rearrange("p t n -> p n t"),
+                gates[b][:],
+                MULT,
+            )
+
+        out_rows = out.rearrange("(m p) s -> p m s", p=P)
+
+        def project(a, b):
+            o_banks[a] = psum_o.tile([P, 2, b - a], F32, name="o")
+            for m in range(2):
+                multiply(o_banks[a][:, m, :], "w2", m, "z", a, b)
+
+        def leave(a, b, engine):
+            result = keep.tile([P, 2, b - a], F32, name="result%d" % a)
+            copy(engine, result[:], o_banks[a][:])
+            nc.sync.dma_start(out_rows[:, :, a:b], result[:])
+
+        load_plane(3)
+        load_plane(1)
+        load_plane(0)
+        load_plane(2)
+        load_weights("w3")
+        load_edges(0, 256)
+        load_weights("w1")
+        load_edges(256, 512)
+        load_edges(512, 768)
+        load_weights("w2")
+        warm_table()
+        gather_wide(3)
+        gather(1, 0, S)
+        gather(0, 0, S)
+        group_x("S", 0, 2, 0, S)
+        gather_wide(2)
+        quantise("x", 0, 256)
+        group_weights("w3", "S", 0, 80)
+        quantise("x", 256, S)
+        group_weights("w3", "V", 80, 128)
+        group_edges("V", 192, 256)
+        group_edges("S", 0, 192)
+        quantise("w3", 0, H)
+        quantise("e", 0, 256)
+        filter_product(1)
+        group_weights("w1", "S", 0, 32)
+        group_weights("w1", "V", 32, 128)
+        filter_product(0)
+        gate(1)
+        quantise("w1", 0, H)
+        group_edges("S", 256, 384)
+        group_edges("V", 384, 512)
+        atom_product(1)
+        group_edges("V", 576, 768)
+        group_edges("S", 512, 576)
+        atom_product(0)
+        gate(0)
+        quantise("e", 256, 512)
+        atom_product(2)
+        quantise("e", 512, 768)
+        group_weights("w2", "S", 0, 256)
+        filter_product(2)
+        message(1)
+        filter_product(4)
+        message(0)
+        filter_product(3)
+        gate(2)
+        atom_product(4)
+        quantise("w2", 0, N)
+        atom_product(3)
+        quantise("z", 0, 256)
+        gate(4)
+        message(2)
+        filter_product(5)
+        gate(3)
+        project(0, 256)
+        message(4)
+        atom_product(5)
+        gate(5)
+        message(3)
+        leave(0, 256, "S")
+        quantise("z", 512, 640)
+        quantise("z", 256, 512)
+        project(512, 640)
+        message(5)
+        project(256, 512)
+        leave(512, 640, "S")
+        quantise("z", 640, 768)
+        leave(256, 512, "V")
+        project(640, 768)
+        leave(640, 768, "S")

@@ -15,202 +15,216 @@ GELU = mybir.ActivationFunctionType.Gelu_apprx_tanh
 MULT = mybir.AluOpType.mult
 
 P = 128
+PACK = 4
+PAIR = 2
+PIECE = T // 2
+HALF = S // 2
+BANKS = 8
 BLOCK = 128
 
 
 def tile_picked_schnet_gelu_e_kernel(tc, xT, eT, w1, w3, w2, offs, out):
     nc = tc.nc
+    on_scalar, on_vector = nc.scalar.copy, nc.vector.tensor_copy
+
     with ExitStack() as ctx:
         keep = ctx.enter_context(tc.tile_pool(name="keep", bufs=1))
-        psum_f = ctx.enter_context(tc.psum_pool(name="psum_f", bufs=3))
-        psum_c = ctx.enter_context(tc.psum_pool(name="psum_c", bufs=3))
-        psum_o = ctx.enter_context(tc.psum_pool(name="psum_o", bufs=2))
+        psum = ctx.enter_context(tc.psum_pool(name="psum", bufs=BANKS))
+
+        rounded, codes, scales = {}, {}, {}
+        for name, width in (("x", S), ("e", S), ("z", S), ("w1", H), ("w3", H), ("w2", N)):
+            rounded[name] = keep.tile([P, width, PACK], BF16, name="rounded_" + name, align_bytes=64)
+            codes[name] = keep.tile([P, width], U32, name="codes_" + name, align_bytes=64)
+            scales[name] = keep.tile([P, width], U8, name="scales_" + name, align_bytes=64)
+
+        def quantise(name, start, stop):
+            nc.vector.quantize_mx(
+                out=codes[name][:, start:stop].bitcast(FP8X4),
+                scales=scales[name][:, start:stop],
+                in_=rounded[name][:, start:stop, :].rearrange("p w j -> p (w j)"),
+            )
 
         offsets = keep.tile([P, S // 16], U16, name="offsets")
         nc.sync.dma_start(offsets[:], offs)
-        x_rows = xT.rearrange("(p j) t -> p j t", j=4)
-        e_rows = eT.rearrange("(p j) s -> p j s", j=4)
-        weights = {"w1": w1, "w3": w3, "w2": w2}
-        raw, codes, scales, grouped, planes, e_raw = {}, {}, {}, {}, {}, {}
-        f_banks, c_banks, o_banks, gates = {}, {}, {}, {}
 
-        for name, width in (("x", S), ("e", S), ("z", S), ("w1", H), ("w3", H), ("w2", N)):
-            codes[name] = keep.tile([P, width], U32, name="codes_" + name, align_bytes=64)
-            scales[name] = keep.tile([P, width], U8, name="scales_" + name, align_bytes=64)
-            grouped[name] = keep.tile([P, width, 4], BF16, name="grouped_" + name, align_bytes=64)
-        picked = keep.tile([P, 4, S], F32, name="picked", align_bytes=64)
+        x_rows = xT.rearrange("(p u e) t -> p u e t", u=PACK // PAIR, e=PAIR)
+        loaded_pairs = {}
+        for u in range(PACK // PAIR):
+            for first in range(0, T, PIECE):
+                loaded_pairs[u, first] = keep.tile([P, PAIR, PIECE], F32, name="loaded_pairs%d_%d" % (u, first), align_bytes=64)
+                nc.sync.dma_start(loaded_pairs[u, first][:], x_rows[:, u, :, first : first + PIECE])
 
-        def load_plane(j):
-            planes[j] = keep.tile([P, T], F32, name="plane%d" % j, align_bytes=64)
-            nc.sync.dma_start(planes[j][:], x_rows[:, j, :])
+        loaded = {}
 
-        def load_edges(a, b):
-            e_raw[a] = keep.tile([P, 4, b - a], F32, name="e_raw%d" % a, align_bytes=64)
-            nc.sync.dma_start(e_raw[a][:], e_rows[:, :, a:b])
+        def load(name, rows):
+            loaded[name] = keep.tile([P, PACK, rows.shape[1]], F32, name="loaded_" + name, align_bytes=64)
+            nc.sync.dma_start(loaded[name][:], rows.rearrange("(p j) w -> p j w", j=PACK))
 
-        def load_weights(name):
-            raw[name] = keep.tile([P, 4, weights[name].shape[1]], F32, name="raw_" + name, align_bytes=64)
-            nc.sync.dma_start(raw[name][:], weights[name].rearrange("(p j) h -> p j h", j=4))
+        load("w3", w3)
+        load("e_low", eT[:, 0:HALF])
+        load("w1", w1)
+        load("e_high", eT[:, HALF:S])
+        load("w2", w2)
 
-        def warm_table():
-            dummy = keep.tile([P, 1], F32, name="dummy")
-            nc.gpsimd.memset(dummy[:], 0.0)
-            dummy_out = keep.tile([P, 1], F32, name="dummy_out")
-            nc.scalar.activation(dummy_out[:], dummy[:], GELU)
+        zero = keep.tile([P, 1], F32, name="zero")
+        nc.gpsimd.memset(zero[:], 0.0)
+        unused = keep.tile([P, 1], F32, name="unused")
+        nc.scalar.activation(unused[:], zero[:], GELU)
 
-        def copy(engine, dst, src):
-            if engine == "S":
-                nc.scalar.copy(dst, src)
-            elif engine == "V":
-                nc.vector.tensor_copy(dst, src)
-            else:
-                nc.gpsimd.tensor_copy(dst, src)
-
-        def picks(a, b):
-            return offsets[:] if (a, b) == (0, S) else offsets[:, a // 16 : b // 16]
-
-        def gather(j, a, b):
-            nc.vector.tensor_copy(picked[:, j, a:b], planes[j][:].indirect(picks(a, b)))
-
-        def gather_wide(j):
-            nc.vector.tensor_copy(grouped["x"][:, :, j], planes[j][:].indirect(offsets[:]))
-
-        def group_x(engine, j0, j1, a, b):
-            copy(engine, grouped["x"][:, a:b, j0:j1], picked[:, j0:j1, a:b].rearrange("p j n -> p n j"))
-
-        def group_weights(name, engine, a, b):
-            if name == "w2":
-                copy(engine, grouped[name][:, a:b, :], raw[name][:, :, a:b].rearrange("p j n -> p n j"))
-            else:
-                dst = grouped[name][:].rearrange("p (t m) j -> p m t j", t=4)
-                src = raw[name][:].rearrange("p j (m t) -> p m t j", t=4)
-                copy(engine, dst[:, a:b], src[:, a:b])
-
-        def group_edges(engine, a, b):
-            start = max(s for s in e_raw if s <= a)
-            copy(engine, grouped["e"][:, a:b, :], e_raw[start][:, :, a - start : b - start].rearrange("p j n -> p n j"))
-
-        def quantise(name, a, b):
-            nc.vector.quantize_mx(
-                out=codes[name][:, a:b].bitcast(FP8X4),
-                scales=scales[name][:, a:b],
-                in_=grouped[name][:, a:b, :].rearrange("p w j -> p (w j)"),
+        def round_columns(copy, name, source, start, stop, source_start=0):
+            columns = source[:, :, start - source_start : stop - source_start]
+            copy(
+                rounded[name][:, start:stop, :].rearrange("p (c i) j -> p c j i", i=4),
+                columns.rearrange("p j (c i) -> p c j i", i=4),
             )
 
-        def multiply(bank, w, t, x, a, b):
-            chans = slice(t * P, (t + 1) * P)
+        def round_permuted(copy, name, start, stop):
+            copy(
+                rounded[name][:].rearrange("p (t m) j -> p m j t", t=PACK)[:, start:stop],
+                loaded[name][:].rearrange("p j (m t) -> p m j t", t=PACK)[:, start:stop],
+            )
+
+        pairs = [keep.tile([P, T, PAIR], BF16, name="pairs%d" % u, align_bytes=64) for u in range(PACK // PAIR)]
+
+        def round_pairs(copy, u, start, stop):
+            first = start // PIECE * PIECE
+            copy(
+                pairs[u][:, start:stop, :].rearrange("p (c i) e -> p c e i", i=4),
+                loaded_pairs[u, first][:, :, start - first : stop - first].rearrange("p e (c i) -> p c e i", i=4),
+            )
+
+        def gather(u, start, stop):
+            window = pairs[u][:].rearrange("p t e -> p (t e)").bitcast(U32)
+            words = rounded["x"][:].rearrange("p w j -> p (w j)").bitcast(U32).rearrange("p (w u) -> p w u", u=PACK // PAIR)
+            nc.vector.tensor_copy(words[:, start:stop, u], window.indirect(offsets[:, start // 16 : stop // 16]))
+
+        def product(bank, weights, chunk, moving, start, stop):
+            columns = slice(chunk * P, (chunk + 1) * P)
             nc.tensor.matmul_mx(
                 out=bank,
-                lhsT=codes[w][:, chans].bitcast(FP8X4),
-                lhsT_scale=scales[w][:, chans],
-                rhs=codes[x][:, a:b].bitcast(FP8X4),
-                rhs_scale=scales[x][:, a:b],
+                lhsT=codes[weights][:, columns].bitcast(FP8X4),
+                lhsT_scale=scales[weights][:, columns],
+                rhs=codes[moving][:, start:stop].bitcast(FP8X4),
+                rhs_scale=scales[moving][:, start:stop],
                 start=True,
                 stop=True,
             )
 
-        def filter_product(b):
-            f_banks[b] = psum_f.tile([P, 4, BLOCK], F32, name="f")
-            for t in range(4):
-                multiply(f_banks[b][:, t, :], "w3", t, "e", b * BLOCK, (b + 1) * BLOCK)
+        def first_product(weights, moving, b):
+            bank = psum.tile([P, PACK, BLOCK], F32, name="bank")
+            for t in range(PACK):
+                product(bank[:, t, :], weights, t, moving, b * BLOCK, (b + 1) * BLOCK)
+            return bank
 
-        def atom_product(b):
-            c_banks[b] = psum_c.tile([P, 4, BLOCK], F32, name="c")
-            for t in range(4):
-                multiply(c_banks[b][:, t, :], "w1", t, "x", b * BLOCK, (b + 1) * BLOCK)
+        filtered, atom, gates = {}, {}, {}
+
+        def filters(b):
+            filtered[b] = first_product("w3", "e", b)
+
+        def atoms(b):
+            atom[b] = first_product("w1", "x", b)
 
         def gate(b):
-            gates[b] = keep.tile([P, BLOCK, 4], F32, name="gate%d" % b, align_bytes=64)
-            nc.scalar.activation(gates[b][:], f_banks[b][:].rearrange("p t n -> p n t"), GELU)
+            gates[b] = keep.tile([P, BLOCK, PACK], F32, name="gate%d" % b, align_bytes=64)
+            nc.scalar.activation(gates[b][:], filtered[b][:].rearrange("p t n -> p n t"), GELU)
 
         def message(b):
             nc.vector.tensor_tensor(
-                grouped["z"][:, b * BLOCK : (b + 1) * BLOCK, :],
-                c_banks[b][:].rearrange("p t n -> p n t"),
-                gates[b][:],
-                MULT,
+                rounded["z"][:, b * BLOCK : (b + 1) * BLOCK, :], atom[b][:].rearrange("p t n -> p n t"), gates[b][:], MULT
             )
 
         out_rows = out.rearrange("(m p) s -> p m s", p=P)
+        last = {}
 
-        def project(a, b):
-            o_banks[a] = psum_o.tile([P, 2, b - a], F32, name="o")
-            for m in range(2):
-                multiply(o_banks[a][:, m, :], "w2", m, "z", a, b)
+        def project(start, stop):
+            last[start] = psum.tile([P, N // P, stop - start], F32, name="bank")
+            for m in range(N // P):
+                product(last[start][:, m, :], "w2", m, "z", start, stop)
 
-        def leave(a, b, engine):
-            result = keep.tile([P, 2, b - a], F32, name="result%d" % a)
-            copy(engine, result[:], o_banks[a][:])
-            nc.sync.dma_start(out_rows[:, :, a:b], result[:])
+        def leave(copy, start, stop):
+            result = keep.tile([P, N // P, stop - start], F32, name="result%d" % start)
+            copy(result[:], last[start][:])
+            nc.sync.dma_start(out_rows[:, :, start:stop], result[:])
 
-        load_plane(3)
-        load_plane(1)
-        load_plane(0)
-        load_plane(2)
-        load_weights("w3")
-        load_edges(0, 256)
-        load_weights("w1")
-        load_edges(256, 512)
-        load_edges(512, 768)
-        load_weights("w2")
-        warm_table()
-        gather_wide(3)
-        gather(1, 0, S)
-        gather(0, 0, S)
-        group_x("S", 0, 2, 0, S)
-        gather_wide(2)
-        quantise("x", 0, 256)
-        group_weights("w3", "S", 0, 80)
-        quantise("x", 256, S)
-        group_weights("w3", "V", 80, 128)
-        group_edges("V", 192, 256)
-        group_edges("S", 0, 192)
+        def project_apart(start, stop):
+            for m in range(N // P):
+                last[start, m] = psum.tile([P, stop - start], F32, name="bank")
+                product(last[start, m][:], "w2", m, "z", start, stop)
+
+        def leave_apart(copy, m, start, stop):
+            result = keep.tile([P, stop - start], F32, name="result%d_%d" % (start, m))
+            copy(result[:], last[start, m][:])
+            nc.sync.dma_start(out_rows[:, m, start:stop], result[:])
+
+
+        round_pairs(on_scalar, 0, 0, 1024)
+        round_pairs(on_vector, 0, 1536, 2048)
+        round_pairs(on_scalar, 0, 1024, 1536)
+        gather(0, 0, 512)
+        round_pairs(on_scalar, 1, 0, 768)
+        gather(0, 512, S)
+        round_pairs(on_vector, 1, 768, 1024)
+        round_pairs(on_vector, 1, 1408, 2048)
+        round_pairs(on_scalar, 1, 1024, 1408)
+        gather(1, 0, 512)
+
+        round_permuted(on_scalar, "w3", 0, 80)
+        round_permuted(on_vector, "w3", 80, 128)
+        quantise("x", 0, 512)
+        gather(1, 512, S)
+        round_columns(on_scalar, "e", loaded["e_low"], 0, 128)
         quantise("w3", 0, H)
-        quantise("e", 0, 256)
-        filter_product(1)
-        group_weights("w1", "S", 0, 32)
-        group_weights("w1", "V", 32, 128)
-        filter_product(0)
-        gate(1)
-        quantise("w1", 0, H)
-        group_edges("S", 256, 384)
-        group_edges("V", 384, 512)
-        atom_product(1)
-        group_edges("V", 576, 768)
-        group_edges("S", 512, 576)
-        atom_product(0)
+        round_columns(on_scalar, "e", loaded["e_low"], 128, HALF)
+        quantise("e", 0, 128)
+        quantise("x", 512, S)
+
+        filters(0)
+        quantise("e", 128, HALF)
+        round_permuted(on_scalar, "w1", 0, 32)
+        round_permuted(on_vector, "w1", 32, 128)
+        filters(1)
         gate(0)
-        quantise("e", 256, 512)
-        atom_product(2)
-        quantise("e", 512, 768)
-        group_weights("w2", "S", 0, 256)
-        filter_product(2)
-        message(1)
-        filter_product(4)
-        message(0)
-        filter_product(3)
+        filters(2)
+        quantise("w1", 0, H)
+        gate(1)
+
+        round_columns(on_vector, "e", loaded["e_high"], HALF, 640, source_start=HALF)
+        atoms(0)
+        round_columns(on_scalar, "e", loaded["e_high"], 640, S, source_start=HALF)
+        atoms(1)
+        quantise("e", HALF, 640)
         gate(2)
-        atom_product(4)
-        quantise("w2", 0, N)
-        atom_product(3)
-        quantise("z", 0, 256)
-        gate(4)
+        quantise("e", 640, S)
+        atoms(2)
+
+        message(0)
+        round_columns(on_scalar, "w2", loaded["w2"], 0, N)
+        filters(3)
+        message(1)
+        atoms(3)
+        atoms(4)
         message(2)
-        filter_product(5)
         gate(3)
+        filters(4)
+        quantise("z", 0, 256)
+        filters(5)
+        message(3)
+        atoms(5)
+        gate(4)
+        quantise("w2", 0, N)
+        gate(5)
+        quantise("z", 256, 512)
         project(0, 256)
         message(4)
-        atom_product(5)
-        gate(5)
-        message(3)
-        leave(0, 256, "S")
-        quantise("z", 512, 640)
-        quantise("z", 256, 512)
-        project(512, 640)
-        message(5)
         project(256, 512)
-        leave(512, 640, "S")
-        quantise("z", 640, 768)
-        leave(256, 512, "V")
-        project(640, 768)
-        leave(640, 768, "S")
+        message(5)
+
+        leave(on_scalar, 0, 256)
+        quantise("z", 512, 640)
+        leave(on_scalar, 256, 512)
+        quantise("z", 640, S)
+        project_apart(512, 640)
+        project(640, S)
+        leave_apart(on_scalar, 0, 512, 640)
+        leave_apart(on_vector, 1, 512, 640)
+        leave(on_vector, 640, S)

from contextlib import ExitStack

import concourse.mybir as mybir

K, T, S, J, H, N = 512, 2048, 768, 512, 512, 256
FLOPS = 2 * S * (K * H + J * H + H * N)

F32 = mybir.dt.float32
BF16 = mybir.dt.bfloat16
U32 = mybir.dt.uint32
U16 = mybir.dt.uint16
U8 = mybir.dt.uint8
FP8X4 = mybir.dt.float8_e4m3fn_x4
GELU = mybir.ActivationFunctionType.Gelu_apprx_tanh
MULT = mybir.AluOpType.mult

P = 128
PACK = 4
PAIR = 2
PIECE = T // 2
HALF = S // 2
BANKS = 8
BLOCK = 128


def tile_picked_schnet_gelu_e_kernel(tc, xT, eT, w1, w3, w2, offs, out):
    nc = tc.nc
    on_scalar, on_vector = nc.scalar.copy, nc.vector.tensor_copy

    with ExitStack() as ctx:
        keep = ctx.enter_context(tc.tile_pool(name="keep", bufs=1))
        psum = ctx.enter_context(tc.psum_pool(name="psum", bufs=BANKS))

        rounded, codes, scales = {}, {}, {}
        for name, width in (("x", S), ("e", S), ("z", S), ("w1", H), ("w3", H), ("w2", N)):
            rounded[name] = keep.tile([P, width, PACK], BF16, name="rounded_" + name, align_bytes=64)
            codes[name] = keep.tile([P, width], U32, name="codes_" + name, align_bytes=64)
            scales[name] = keep.tile([P, width], U8, name="scales_" + name, align_bytes=64)

        def quantise(name, start, stop):
            nc.vector.quantize_mx(
                out=codes[name][:, start:stop].bitcast(FP8X4),
                scales=scales[name][:, start:stop],
                in_=rounded[name][:, start:stop, :].rearrange("p w j -> p (w j)"),
            )

        offsets = keep.tile([P, S // 16], U16, name="offsets")
        nc.sync.dma_start(offsets[:], offs)

        x_rows = xT.rearrange("(p u e) t -> p u e t", u=PACK // PAIR, e=PAIR)
        loaded_pairs = {}
        for u in range(PACK // PAIR):
            for first in range(0, T, PIECE):
                loaded_pairs[u, first] = keep.tile([P, PAIR, PIECE], F32, name="loaded_pairs%d_%d" % (u, first), align_bytes=64)
                nc.sync.dma_start(loaded_pairs[u, first][:], x_rows[:, u, :, first : first + PIECE])

        loaded = {}

        def load(name, rows):
            loaded[name] = keep.tile([P, PACK, rows.shape[1]], F32, name="loaded_" + name, align_bytes=64)
            nc.sync.dma_start(loaded[name][:], rows.rearrange("(p j) w -> p j w", j=PACK))

        load("w3", w3)
        load("e_low", eT[:, 0:HALF])
        load("w1", w1)
        load("e_high", eT[:, HALF:S])
        load("w2", w2)

        zero = keep.tile([P, 1], F32, name="zero")
        nc.gpsimd.memset(zero[:], 0.0)
        unused = keep.tile([P, 1], F32, name="unused")
        nc.scalar.activation(unused[:], zero[:], GELU)

        def round_columns(copy, name, source, start, stop, source_start=0):
            columns = source[:, :, start - source_start : stop - source_start]
            copy(
                rounded[name][:, start:stop, :].rearrange("p (c i) j -> p c j i", i=4),
                columns.rearrange("p j (c i) -> p c j i", i=4),
            )

        def round_permuted(copy, name, start, stop):
            copy(
                rounded[name][:].rearrange("p (t m) j -> p m j t", t=PACK)[:, start:stop],
                loaded[name][:].rearrange("p j (m t) -> p m j t", t=PACK)[:, start:stop],
            )

        pairs = [keep.tile([P, T, PAIR], BF16, name="pairs%d" % u, align_bytes=64) for u in range(PACK // PAIR)]

        def round_pairs(copy, u, start, stop):
            first = start // PIECE * PIECE
            copy(
                pairs[u][:, start:stop, :].rearrange("p (c i) e -> p c e i", i=4),
                loaded_pairs[u, first][:, :, start - first : stop - first].rearrange("p e (c i) -> p c e i", i=4),
            )

        def gather(u, start, stop):
            window = pairs[u][:].rearrange("p t e -> p (t e)").bitcast(U32)
            words = rounded["x"][:].rearrange("p w j -> p (w j)").bitcast(U32).rearrange("p (w u) -> p w u", u=PACK // PAIR)
            nc.vector.tensor_copy(words[:, start:stop, u], window.indirect(offsets[:, start // 16 : stop // 16]))

        def product(bank, weights, chunk, moving, start, stop):
            columns = slice(chunk * P, (chunk + 1) * P)
            nc.tensor.matmul_mx(
                out=bank,
                lhsT=codes[weights][:, columns].bitcast(FP8X4),
                lhsT_scale=scales[weights][:, columns],
                rhs=codes[moving][:, start:stop].bitcast(FP8X4),
                rhs_scale=scales[moving][:, start:stop],
                start=True,
                stop=True,
            )

        def first_product(weights, moving, b):
            bank = psum.tile([P, PACK, BLOCK], F32, name="bank")
            for t in range(PACK):
                product(bank[:, t, :], weights, t, moving, b * BLOCK, (b + 1) * BLOCK)
            return bank

        filtered, atom, gates = {}, {}, {}

        def filters(b):
            filtered[b] = first_product("w3", "e", b)

        def atoms(b):
            atom[b] = first_product("w1", "x", b)

        def gate(b):
            gates[b] = keep.tile([P, BLOCK, PACK], F32, name="gate%d" % b, align_bytes=64)
            nc.scalar.activation(gates[b][:], filtered[b][:].rearrange("p t n -> p n t"), GELU)

        def message(b):
            nc.vector.tensor_tensor(
                rounded["z"][:, b * BLOCK : (b + 1) * BLOCK, :], atom[b][:].rearrange("p t n -> p n t"), gates[b][:], MULT
            )

        out_rows = out.rearrange("(m p) s -> p m s", p=P)
        last = {}

        def project(start, stop):
            last[start] = psum.tile([P, N // P, stop - start], F32, name="bank")
            for m in range(N // P):
                product(last[start][:, m, :], "w2", m, "z", start, stop)

        def leave(copy, start, stop):
            result = keep.tile([P, N // P, stop - start], F32, name="result%d" % start)
            copy(result[:], last[start][:])
            nc.sync.dma_start(out_rows[:, :, start:stop], result[:])

        def project_apart(start, stop):
            for m in range(N // P):
                last[start, m] = psum.tile([P, stop - start], F32, name="bank")
                product(last[start, m][:], "w2", m, "z", start, stop)

        def leave_apart(copy, m, start, stop):
            result = keep.tile([P, stop - start], F32, name="result%d_%d" % (start, m))
            copy(result[:], last[start, m][:])
            nc.sync.dma_start(out_rows[:, m, start:stop], result[:])


        round_pairs(on_scalar, 0, 0, 1024)
        round_pairs(on_vector, 0, 1536, 2048)
        round_pairs(on_scalar, 0, 1024, 1536)
        gather(0, 0, 512)
        round_pairs(on_scalar, 1, 0, 768)
        gather(0, 512, S)
        round_pairs(on_vector, 1, 768, 1024)
        round_pairs(on_vector, 1, 1408, 2048)
        round_pairs(on_scalar, 1, 1024, 1408)
        gather(1, 0, 512)

        round_permuted(on_scalar, "w3", 0, 80)
        round_permuted(on_vector, "w3", 80, 128)
        quantise("x", 0, 512)
        gather(1, 512, S)
        round_columns(on_scalar, "e", loaded["e_low"], 0, 128)
        quantise("w3", 0, H)
        round_columns(on_scalar, "e", loaded["e_low"], 128, HALF)
        quantise("e", 0, 128)
        quantise("x", 512, S)

        filters(0)
        quantise("e", 128, HALF)
        round_permuted(on_scalar, "w1", 0, 32)
        round_permuted(on_vector, "w1", 32, 128)
        filters(1)
        gate(0)
        filters(2)
        quantise("w1", 0, H)
        gate(1)

        round_columns(on_vector, "e", loaded["e_high"], HALF, 640, source_start=HALF)
        atoms(0)
        round_columns(on_scalar, "e", loaded["e_high"], 640, S, source_start=HALF)
        atoms(1)
        quantise("e", HALF, 640)
        gate(2)
        quantise("e", 640, S)
        atoms(2)

        message(0)
        round_columns(on_scalar, "w2", loaded["w2"], 0, N)
        filters(3)
        message(1)
        atoms(3)
        atoms(4)
        message(2)
        gate(3)
        filters(4)
        quantise("z", 0, 256)
        filters(5)
        message(3)
        atoms(5)
        gate(4)
        quantise("w2", 0, N)
        gate(5)
        quantise("z", 256, 512)
        project(0, 256)
        message(4)
        project(256, 512)
        message(5)

        leave(on_scalar, 0, 256)
        quantise("z", 512, 640)
        leave(on_scalar, 256, 512)
        quantise("z", 640, S)
        project_apart(512, 640)
        project(640, S)
        leave_apart(on_scalar, 0, 512, 640)
        leave_apart(on_vector, 1, 512, 640)
        leave(on_vector, 640, S)
